import numpy as np, ml_dtypes
CORES = [16,17,18,19,32,33,34,35]
N = 8
BF = ml_dtypes.bfloat16
W, L, Q, PARTS, TH, AC, T = 4096, 512, 8, 4, 64, 6, 3
S, H, LB = 512, 2048, 12
def parts(rng):
    amp = rng.choice(np.array([176, 208, 256]), (N, 8, 1, 1)); lo = ((257 - amp) * rng.random((N, 8, 1, 1))).astype(np.int64)
    x = lo + (amp * rng.random((N, 8, 16, W), dtype=np.float32)).astype(np.int64)
    return np.minimum(x, 255), rng.integers(0, W, (N, 8, 16, W)), rng.integers(0, W, (N, 8, 16, L)), rng.integers(0, 64, (N, 8, 16))
def pack(x, b, c, w):
    return {"x": x.reshape(N, 128, W).astype(np.float32).astype(BF), "pk": (b[..., :H] + W * b[..., H:]).reshape(N, 128, H).astype(np.int32),
            "cb": c.reshape(N, 128, L).astype(np.int32), "wt": w.reshape(N, 128, 1).astype(np.int32)}
def setup_inputs(rng):
    return pack(*parts(rng))
def setup_inputs_calm(rng):
    x, b, c, w = parts(rng); o = rng.permutation(8); k = np.arange(16)[:, None]
    for g in o[:3]:
        x[:, g] = int(rng.integers(0, 256 - TH)) + rng.integers(0, TH + 1, (N, 16, W))
    g = o[3]; s = rng.integers(0, 16, (N, 16, W))
    x[:, g] = np.where(np.arange(W) >= H, 255 - s, s)
    c[:, g] = rng.integers(0, H, (N, 16, L)) + H * (k % 2); b[:, g] = rng.integers(0, H, (N, 16, W)) + H * (k % 2)
    q = int(rng.integers(0, N))
    for g in o[3:]:
        x[q, g] = int(rng.integers(0, 256 - TH)) + rng.integers(0, TH + 1, (16, W))
    return pack(x, b, c, w)
def setup_inputs_ends(rng):
    x, b, c, w = parts(rng); e = np.array([0, 1, H - 1, H, W - 2, W - 1])
    c[:, 0] = rng.choice(e, (N, 16, L)); b[:, 0] = rng.choice(e, (N, 16, W))
    c[:, 1] = rng.integers(0, W, (N, 1, L)); c[:, 2] = rng.integers(0, W, (N, 16, 1))
    b[:, 3] = np.arange(W); w[:, 4] = 0; w[:, 5] = 63
    x[:, 5] = 255 * (rng.random((N, 16, W)) < 0.85); x[1::2, 5] = rng.integers(200, 256, (N // 2, 16, W))
    x[:, 6] |= 15; w[:, 7, :15] = 0; w[:, 7, 15] = rng.integers(1, 64, N)
    return pack(x, b, c, w)
def setup_inputs_heavy(rng):
    x, b, c, w = parts(rng); k = np.arange(16)[:, None]; q = int(rng.integers(0, N)); A = 15 * (L - 1)
    s = rng.integers(0, 16, (N, 8, 16, W)); x = np.where(np.arange(W) >= H, 255 - s, s)
    c = rng.integers(16, H, (N, 8, 16, L)) + H * (k % 2); b = rng.integers(16, H, (N, 8, 16, W)) + H * (k % 2)
    for g in range(8):
        p = rng.permutation(16); j = int(rng.integers(1, 15))
        if g % 4 < 2:
            hs = np.arange(227700, 240900); hs = hs[((37 * hs + A) & (2 * W - 1)) == (W, 2 * W - 1)[g % 4]]; h = int(rng.choice(hs))
            last = 192 + (h - 192) % 63; a = (h - last) // 63
            u = rng.permutation(np.repeat(np.arange(15), 15))[:a - 3600]
            val = np.insert(240 + np.bincount(u, minlength=15), j, last); w[q, g] = 63; w[q, g, j] = 1
        elif g % 4 == 2:
            val = rng.integers(0, 16, 16); val[j] = 255
        else:
            val = int(rng.integers(0, 256 - TH)) + rng.integers(0, TH + 1, 16)
        x[q, g][:, p] = val; c[q, g, :, 1 + PARTS * int(rng.integers(0, L // PARTS))] = p
    return pack(x, b, c, w)
def setup_inputs_ties(rng):
    x, b, c, w = parts(rng)
    for r in range(N):
        for g in range(0, 8, 2):
            o = rng.permutation(W); cl = np.zeros(W, np.int64); cl[o[W // 3:2 * (W // 3)]] = 1; cl[o[2 * (W // 3):]] = 2
            lo = int(rng.integers(0, 255 - TH)); x[r, g] = np.array([lo, lo + TH, lo + TH + 1])[cl][None, :]
            n = rng.choice(np.array([0, 1, AC - 1, AC, AC + 1, 15]), L)
            if r == 0 and g == 0: n[:] = AC
            if r == 0 and g == 2: n[:] = AC + 1
            cr = np.zeros((17, L), bool); cr[1:16] = np.argsort(np.argsort(rng.random((15, L)), axis=0), axis=0) < n
            s = 2 * ((np.add.accumulate(cr[:16].astype(np.int64), axis=0) + rng.integers(0, 2, L)) % 2)
            s = np.where(~cr[:16] & ~cr[1:] & (rng.random((16, L)) < 0.5), 1, s)
            for a in range(3):
                mem = np.flatnonzero(cl == a); c[r, g] = np.where(s == a, mem[rng.integers(0, mem.size, (16, L))], c[r, g])
    return pack(x, b, c, w)
def setup_inputs_spread(rng):
    x, b, c, w = parts(rng); lo = rng.choice(np.array([0.0, 5.0, 7.0]), (N, 8, 1, 1))
    x = np.minimum((np.exp2(lo + (8 - lo) * rng.random((N, 8, 1, W))) * rng.random((N, 8, 16, W))).astype(np.int64), 255)
    x = np.where(rng.random((N, 8, 1, W)) < 0.25, 255 - x, x)
    c = np.minimum((W * rng.random((N, 8, 16, L)) ** 3).astype(np.int64), W - 1); b = np.minimum((W * rng.random((N, 8, 16, W)) ** 2).astype(np.int64), W - 1)
    w = np.minimum(np.exp2(6 * rng.random((N, 8, 16))).astype(np.int64), 63)
    return pack(x, b, c, w)
def check_inputs(d):
    bad = []
    for k, hi in (("x", 255), ("pk", W * W - 1), ("cb", W - 1), ("wt", 63)):
        a = np.asarray(d[k]).astype(np.float64)
        if not np.all((a >= 0) & (a <= hi) & (a == np.floor(a))): bad.append("range of " + k)
    return bad
def reference(x, pk, cb, wt):
    X = x.astype(np.float32).astype(np.int64).reshape(N, 8, 16, W); p = pk.astype(np.int64).reshape(N, 8, 16, H)
    B = np.concatenate([p & (W - 1), p >> LB], axis=3)
    c = cb.astype(np.int64).reshape(N, 8, 16, L); w = wt.astype(np.int64).reshape(N, 8, 16, 1)
    lane = np.arange(L); rr = np.arange(N)[:, None, None, None]; gg = np.arange(8)[None, :, None, None]
    for t in range(T):
        e = np.take_along_axis(X, c, 3)
        z = np.concatenate([np.zeros((N, 8, 1, L), np.int64), e[:, :, :15] & 15], axis=2)
        v = X[rr, gg, z, c]
        cr = np.concatenate([np.zeros((N, 8, 1, L), bool), np.abs(v[:, :, 1:] - v[:, :, :15]) > TH], axis=2)
        n = np.add.reduce(cr.astype(np.int64), axis=2); A = np.add.reduce(n, axis=2)[:, :, None]; h = np.add.reduce(w * v, axis=2)
        ok = n <= AC; place = S * ((h + A) & (Q - 1)) + lane; nxt = (37 * h + A) & (W - 1)
        mend = np.where(cr, np.take_along_axis(B, c, 3), c)
        X, B = np.array(X), np.array(B)
        for r in range(N):
            for m in range(PARTS):
                q = r if m == 0 else (r + 1 + (t + m - 1) % (N - 1)) % N
                for g in range(8):
                    i = lane[m::PARTS]; i = i[ok[r, g, i]]
                    X[q, g][:, place[r, g, i]] = v[r, g][:, i]; B[q, g][:, place[r, g, i]] = c[r, g][:, i]
        new = np.take_along_axis(B, np.repeat(nxt[:, :, None, :], 16, axis=2), 3)
        c = np.where(ok[:, :, None, :], new, mend)
    return {"yx": X.reshape(N, 128, W).astype(np.float32).astype(BF), "yc": c.reshape(N, 128, L).astype(np.float32)}

from concourse.bass import DstId, RemoteDMATransfer
from concourse.mybir import AluOpType as ALU, ActivationFunctionType as AF

NR = 3
MINS = 4
SLOTS = ((1, 2, 3, 4), (5, 6, 7), (8, 9, 10, 11), (12, 13, 14, 15))
XV = ((0, 1), (2, 1))
THS = (2,)
BCH = 64
ORDER = [1, 2, 3, 0]
BON = {"v3": 1.8, "s30": 4.9, "t1": 5.7, "x00": -2.3, "x01": -2.3, "x10": -2.3, "x11": -2.3, "x20": -2.8, "x21": -2.8,
       "x30": -2.3, "x31": -2.3, "s02": 6.9, "d13": 0.5, "d33": 4.3, "s33": 3.5, "d00": 5.9, "d01": 0.1, "d02": 5.9,
       "d03": 5.9, "s03": 3.8, "t0": 5.3, "d31": -1.3, "s20": -4.5, "s22": 4.5, "d22": 6.5, "d20": 1.4, "d21": 1.4,
       "d23": 1.4, "s31": 4.2, "s32": 4.2, "d30": -1.0, "b6": 1.0}
LOOK = 0.15
CY, GA, SC, TE, NL = 0.00083 * 1.1, 1.56, 3.8, 0.00045, 1.0
CAP = None

SCRATCH = {}
for _spec in (
        "XT 8192 bfloat16, BT 8704 int32, PK 2048 int32, CBI 512 int32, WTI 1 int32, WTF 1 float32, G 8192 bfloat16, "
        "GB 8192 float16, CF 512 float16, R 8192 bfloat16, TH 1024 bfloat16, Z 1024 bfloat16, AB 512 bfloat16, "
        "SG 512 bfloat16, ACC 4 float32, X2S 512 float32, YW 320 int32, YC 512 float32, IOC 144 int32, IOP 1 int32, "
        "SI 32 int32, II 32 int32, PI 8 int32, PF 8 float32, DC 24 float32, CI 576 int32, IOF 144 float32, "
        "KF 1280 float32, RM 16 float32, RM8 8 float32, RMA 8 float32, S1 144 bfloat16, LW 144 bfloat16, "
        "QB 144 bfloat16, RZ 128 bfloat16, IDB 128 bfloat16, DX 1920 bfloat16, ZB 128 bfloat16, KB 128 bfloat16, "
        "ZL 2048 bfloat16, GC 128 bfloat16, DF 128 bfloat16, BO 128 float32, CA 128 bfloat16, CC 128 bfloat16, "
        "ONE 128 bfloat16, DB 2048 bfloat16, I16 128 float16, PP 128 bfloat16, PN 128 bfloat16").split(", ") + [
        "%s%d %s" % (n, t, d) for t in range(NR) for n, d in (
            ("C", "512 uint16"), ("V", "512 bfloat16"), ("OF", "32 uint16"), ("NX", "32 uint16"),
            ("CIN", "384 uint16"), ("VIN", "384 bfloat16"), ("OIN", "24 uint16"))]:
    _n, _w, _d = _spec.split()
    SCRATCH[_n] = ("sbuf", [128, int(_w)], _d)
BANKS = ["e0", "e1", "d0", "d1", "d2", "d3", "v0", "v1"]
for _n in BANKS:
    SCRATCH[_n] = ("psum", [128, 512], "float32")
DMAS = ["ldc", "ldw", "ldx", "ldp0", "ldp1", "stx", "stc"]
SEMAPHORES = ["qV", "qS", "qP", "qG", "loc"] + DMAS + ["%s%d" % (n, t) for n in ("cin", "vin", "oin") for t in range(NR)]


def shares(pool, n):
    z = len(pool)
    sizes = {1: [z], 2: [z // 2] * 2, 3: [z // 2, z // 4, z // 4]}[n]
    return [pool[sum(sizes[:i]):sum(sizes[:i + 1])] for i in range(n)]


def engine_split(topo, src, dsts):
    lists = [topo.engines(src, d) for d in dsts]
    pool = min(lists, key=len)
    narrow = [i for i in range(len(dsts)) if len(lists[i]) == len(pool)]
    wide = [i for i in range(len(dsts)) if len(lists[i]) > len(pool)]
    got = dict(zip(narrow, shares(pool, len(narrow))))
    if wide:
        got.update(zip(wide, shares([e for e in lists[wide[0]] if e not in pool], len(wide))))
    return [got[i] for i in range(len(dsts))]


def target(r, t, m, n):
    return (r + 1 + ((t + m - 1) % (n - 1))) % n


def rank_program(g, core, T, topo):
    rank = T.rank_of(core)
    if rank is None:
        return
    cores = list(T.cores)
    n_ranks = len(cores)
    ops, hist, sent, cur = [], {}, [0], ["c"]
    vec, act, ten = g.vector, g.scalar, g.tensor

    def note(q, dur, thunks, rd, wr, sem=None, val=0, after=None, lat=0.0):
        idx = len(ops)
        deps = {}
        for w, regs in ((0, rd), (1, wr)):
            for reg in regs:
                b, c0, c1 = reg[0], reg[1], reg[2]
                p0, p1 = (reg[3], reg[4]) if len(reg) > 3 else (0, 128)
                ps = b in BANKS
                keep = []
                for e in hist.get(b, []):
                    j, ew, e0, e1, f0, f1 = e
                    if j == idx:
                        keep.append(e)
                        continue
                    oq = ops[j]["q"]
                    conf = e0 < c1 and c0 < e1 and f0 < p1 and p0 < f1 and (ew or w)
                    if conf or (ps and (oq != q or q == "P")):
                        deps[j] = deps.get(j, False) or oq != q or q != "P"
                    if ps and q == "P":
                        continue
                    if w and not ps and c0 <= e0 and e1 <= c1 and p0 <= f0 and f1 <= p1:
                        continue
                    keep.append(e)
                keep.append((idx, w, c0, c1, p0, p1))
                hist[b] = keep
        if after is not None:
            deps[after] = True
        ops.append({"q": q, "dur": dur, "th": thunks, "deps": deps, "sem": sem, "val": val, "lat": lat, "tag": cur[0]})
        return idx

    def ap(b, c0, c1, step=1, p0=0, p1=128):
        t = T[b]
        if p0 == 0 and p1 == 128:
            return t[:, c0:c1] if step == 1 else t[:, c0:c1:step]
        return t[p0:p1, c0:c1]

    def A(b, c0, c1, step=1):
        return lambda: ap(b, c0, c1, step)

    def ts(out, in0, s1, op0, s2=None, op1=None):
        regs = [in0] + [x for x in (s1, s2) if isinstance(x, tuple)]
        a1, a2 = [ap(*x) if isinstance(x, tuple) else x for x in (s1, s2)]

        def go():
            if op1 is None:
                return vec.tensor_scalar(ap(*out), ap(*in0), a1, None, op0)
            return vec.tensor_scalar(ap(*out), ap(*in0), a1, a2, op0, op1)
        note("V", 0.07 + (out[2] - out[1]) * CY, [(go, True)], regs, [out])

    def tt(out, in0, in1, op, step1=1):
        both = in0[0] not in BANKS and in1[0] not in BANKS
        go = lambda: vec.tensor_tensor(ap(*out), ap(*in0), ap(in1[0], in1[1], in1[2], step1), op)
        note("V", 0.07 + (in0[2] - in0[1]) * CY * (2 if both else 1), [(go, True)], [in0, in1], [out])

    def cp(out, in_, step=1):
        go = lambda: vec.tensor_copy(ap(*out), ap(in_[0], in_[1], in_[2], step))
        note("V", 0.07 + (out[2] - out[1]) * CY, [(go, True)], [in_], [out])

    def fill(reg, val):
        note("V", 0.13, [(lambda: vec.memset(ap(*reg), val), True)], [], [reg])

    def sa(out, in_, func, scale=None, bias=None, acc=None):
        kw = {}
        rd, wr = [in_], [out]
        for name, x in (("scale", scale), ("bias", bias)):
            if isinstance(x, tuple):
                rd.append(x)
                kw[name] = ap(*x)
            elif x is not None:
                kw[name] = x
        if acc is not None:
            wr.append(acc)
            kw["accum_out"] = ap(*acc)

        def full(r):
            return ap(r[0], r[1], r[2], 1, r[3], r[4]) if len(r) > 3 else ap(*r)
        go = lambda: act.activation(full(out), full(in_), func, **kw)
        note("S", 0.09 + (out[2] - out[1]) * CY, [(go, True)], rd, wr)

    def mms(items, rd, wr):
        th, dur = [], 0.03
        for o, l, r, st, sp, n in items:
            th.append((lambda o=o, l=l, r=r, st=st, sp=sp: ten.matmul(o(), l(), r(), st, sp), sp))
            dur += TE * max(64, n) * 1.05
        th[-1] = (th[-1][0], True)
        note("P", dur, th, rd, wr)

    def iota(out, pattern, base, cm):
        n = out[2] - out[1]
        note("G", 0.13 + 2 * n * CY, [(lambda: g.iota(ap(*out), pattern, base, cm), True)], [], [out])

    def load(sem, out, src, us):
        note("Y", 0.1, [(lambda: g.sync.dma_start(ap(*out), src), True)], [], [out], sem=sem, val=16, lat=us)

    def store(sem, out, src, us):
        note("Y", 0.1, [(lambda: g.sync.dma_start(out, ap(*src)), True)], [src], [], sem=sem, val=16, lat=us)

    def gather(eng, out, win, lst, bias=None, outstep=1):
        n = 16 * (lst[2] - lst[1])
        w = lambda: ap(*win).indirect(ap(*lst))
        if eng == "S":
            go = lambda: act.activation(ap(*out), w(), AF.Copy)
        elif bias is None:
            go = lambda: vec.tensor_copy(ap(out[0], out[1], out[2], outstep), w())
        else:
            go = lambda: vec.tensor_scalar(ap(*out), w(), bias, None, ALU.add)
        note(eng, 0.07 + n * CY * GA, [(go, True)], [win, lst], [out])

    def scatter(win, lst, src):
        n = 16 * (lst[2] - lst[1])
        note("V", 0.07 + n * CY * SC, [(lambda: vec.tensor_copy(ap(*win).indirect(ap(*lst)), ap(*src)), True)],
             [lst, src], [win])

    def send(t, kind, src, w, dstname):
        dsts = [cores[target(rank, t, m, n_ranks)] for m in (1, 2, 3)]
        engs = engine_split(topo, core, dsts)

        def go():
            tr = []
            for m in (1, 2, 3):
                rid, pid = topo.addr(dsts[m - 1])[:2]
                mask = sum(1 << e for e in engs[m - 1])
                tr.append(RemoteDMATransfer(dst_ids=[DstId(rid=rid, pnc=pid)], dma_engine_mask=mask,
                                            remote_sem=T.sem["%s%d" % (kind, t)],
                                            src=ap(src, w * m, w * m + w), dst=ap(dstname, w * (m - 1), w * m)))
            sent[0] += sum(len(e) for e in engs)
            return g.remote_dma_fused(tr, local_sem=T.sem.loc)
        i = note("G", 0.6, [(go, False)], [(src, w, 4 * w)], [])
        total = 0
        for m in (1, 2, 3):
            for s in range(n_ranks):
                if target(s, t, m, n_ranks) == rank:
                    ds = [cores[target(s, t, x, n_ranks)] for x in (1, 2, 3)]
                    total += len(engine_split(topo, cores[s], ds)[m - 1])
        note("N", NL * (3.0 if w > 8 else 2.2), [], [], [(dstname, 0, 3 * w)], sem="%s%d" % (kind, t), val=total, after=i)

    def col(j):
        return ("DC", j, j + 1)

    def pf(j):
        return ("PF", j, j + 1)

    def kf(j):
        return ("KF", 128 * j, 128 * j + 128)

    def sq(name):
        return (name, 0, 128)

    load("ldc", ("CBI", 0, 512), T.cb[:], 3.0)
    load("ldw", ("WTI", 0, 1), T.wt[:], 3.0)
    load("ldx", ("XT", 0, 4096), T.x[:], 7.0)
    load("ldp0", ("PK", 0, 1024), T.pk[:, 0:1024], 9.0)
    load("ldp1", ("PK", 1024, 2048), T.pk[:, 1024:2048], 11.0)

    iota(("IOP", 0, 1), [[0, 1]], 0, 1)
    iota(("IOC", 0, 144), [[1, 144]], 0, 0)
    iota(("SI", 0, 32), [[16, 32]], 8192, 1)
    iota(("II", 0, 32), [[1, 4], [64, 8]], 0, 4)
    fill(sq("ONE"), 1.0)
    fill(sq("CC"), 18.0)
    for j, mask in ((0, 127), (1, 15), (2, 112), (3, 56), (4, 7), (5, 64)):
        ts(("PI", j, j + 1), ("IOP", 0, 1), mask, ALU.bitwise_and)
    cp(("PF", 0, 6), ("PI", 0, 6))
    cp(("IOF", 0, 144), ("IOC", 0, 144))
    ts(("CI", 0, 144), ("IOC", 0, 144), -7, ALU.add)
    ts(("CI", 144, 288), ("CI", 0, 144), 63, ALU.bitwise_and)
    cm16, cd16 = ("CI", 288, 416), ("CI", 416, 544)
    ts(cm16, sq("IOC"), 15, ALU.bitwise_and)
    ts(cd16, sq("IOC"), 112, ALU.bitwise_and)
    ts(col(0), pf(2), 0.5, ALU.mult)
    ts(("QB", 0, 135), ("CI", 144, 279), col(0), ALU.is_equal)
    ts(("RM", 0, 16), ("IOF", 0, 16), pf(1), ALU.is_equal)
    for k in range(15):
        kk = k if k < 7 else k - 7
        sa(("DX", 128 * k, 128 * k + 128), ("QB", 7 - kk, 135 - kk), AF.Copy, scale=("RM", k, k + 1))
    for m in range(4):
        cp(("C0", 128 * m, 128 * m + 128), ("CBI", m, 512), step=4)
    ts(sq("CI"), sq("IOC"), 7, ALU.bitwise_and)
    ts(col(1), pf(0), 0.0, ALU.is_equal)
    ts(kf(0), sq("CI"), 7.0, ALU.is_equal, col(1), ALU.mult)
    ts(sq("CA"), kf(0), 18.0, ALU.add)
    ts(col(2), pf(3), 2.0, ALU.mult)
    ts(kf(1), cd16, col(2), ALU.is_equal)
    ts(col(3), pf(5), 32.0, ALU.is_lt)
    ts(col(4), col(3), 512.0, ALU.mult)
    ts(col(5), col(3), 256.0, ALU.mult, -256.0, ALU.add)
    ts(kf(2), cm16, col(4), ALU.mult, col(5), ALU.add)
    tt(sq("ZB"), kf(1), kf(2), ALU.mult)
    ts(("RM8", 0, 8), ("IOF", 0, 8), pf(4), ALU.is_equal)
    ts(col(6), ("RM8", 7, 8), col(3), ALU.mult)
    tt(kf(3), cm16, cm16, ALU.mult)
    ts(kf(3), kf(3), -256.0, ALU.mult, 256.0, ALU.add)
    ts(kf(3), kf(3), col(6), ALU.mult)
    tt(sq("KB"), kf(3), kf(1), ALU.mult)
    ts(col(12), ("RM8", 7, 8), -1.0, ALU.mult, 1.0, ALU.add)
    ts(kf(4), sq("ZB"), col(12), ALU.mult)
    tt(sq("KB"), sq("KB"), kf(4), ALU.add)
    ts(("RMA", 0, 8), ("RM8", 0, 8), col(6), ALU.max)
    for k in range(1, 16):
        if k <= 7:
            sa(("ZL", 128 * k, 128 * k + 128), sq("KB"), AF.Copy, scale=("RMA", k - 1, k))
        else:
            sa(("ZL", 128 * k, 128 * k + 128), sq("ZB"), AF.Copy, scale=("RM8", k - 8, k - 7))
    tt(col(7), pf(1), pf(1), ALU.mult)
    ts(col(8), col(7), -256.0, ALU.mult)
    ts(col(9), pf(2), 15.0, ALU.add)
    ts(col(16), pf(2), 0.0, ALU.mult, -256.0, ALU.add)
    ts(("S1", 0, 143), ("IOF", 0, 143), col(9), ALU.is_equal)
    ts(sq("IDB"), sq("IOF"), pf(0), ALU.is_equal)
    sa(sq("RZ"), sq("IDB"), AF.Copy, scale=("RM", 0, 1))
    ts(col(10), pf(4), 1.0, ALU.add)
    ts(kf(5), cm16, col(10), ALU.is_equal)
    ts(col(11), col(3), -65536.0, ALU.mult, 4096.0, ALU.add)
    ts(col(11), col(11), col(12), ALU.mult)
    ts(kf(5), kf(5), col(11), ALU.mult)
    ts(col(13), col(3), 313088.0, ALU.mult, 256.0, ALU.add)
    ts(col(13), col(13), ("RM8", 7, 8), ALU.mult)
    ts(kf(5), kf(5), col(13), ALU.add)
    ts(kf(6), cm16, 0.5, ALU.is_gt)
    ts(kf(7), cm16, MINS + 0.5, ALU.is_lt)
    tt(kf(7), kf(7), kf(6), ALU.mult)
    tt(kf(7), kf(7), kf(1), ALU.mult)
    tt(sq("GC"), kf(5), kf(7), ALU.mult)
    ts(col(14), pf(0), 1.0, ALU.add)
    ts(kf(8), sq("IOF"), col(14), ALU.is_equal)
    tt(kf(8), sq("IDB"), kf(8), ALU.subtract)
    tt(sq("DF"), kf(8), kf(6), ALU.mult)
    ts(sq("BO"), cd16, pf(2), ALU.is_equal, 0.5, ALU.mult)
    cp(("WTF", 0, 1), ("WTI", 0, 1))
    sa(("LW", 0, 143), ("S1", 0, 143), AF.Copy, scale=("WTF", 0, 1))
    ts(col(15), pf(2), 4.0, ALU.mult)
    ts(("II", 0, 32), ("II", 0, 32), col(15), ALU.subtract)
    ts(("SI", 0, 32), ("SI", 0, 32), pf(2), ALU.subtract)
    for c in (0, 1024):
        ts(("BT", 512 + c, 1536 + c), ("PK", c, c + 1024), 4095, ALU.bitwise_and)
        ts(("BT", 2560 + c, 3584 + c), ("PK", c, c + 1024), 12, ALU.logical_shift_right)
    for k in range(16):
        sa(("DB", 128 * k, 128 * k + 128), sq("IDB"), AF.Copy, scale=("RM", k, k + 1))
    cp(sq("I16"), sq("IDB"))
    sa(sq("PP"), sq("IDB"), AF.Copy, scale=2048.0)
    sa(sq("PN"), sq("IDB"), AF.Copy, scale=-2048.0)

    for t in range(NR):
        C, V, OF, NX = "C%d" % t, "V%d" % t, "OF%d" % t, "NX%d" % t
        cur[0] = "c"
        send(t, "cin", C, 128, "CIN%d" % t)
        for q in range(4):
            m = ORDER[q]
            s0, j0, z0, r0 = 128 * m, 2048 * m, 256 * q, 2048 * q
            for h in range(2):
                cur[0] = "x%d%d" % (q, h)
                gather("V" if (q, h) in XV else "S", ("G", j0 + 1024 * h, j0 + 1024 * h + 1024), ("XT", 0, 4096),
                       (C, s0 + 64 * h, s0 + 64 * h + 64))
            E, VB = BANKS[q % 2], BANKS[6 + q % 2]
            cur[0] = "e%d" % q
            it = [(A(E, 0, 128), A("CA", 0, 128), A("ONE", 0, 128), True, False, 128)]
            for k in range(15):
                if k == 7:
                    it.append((A(E, 128, 256), A("CC", 0, 128), A("ONE", 0, 128), True, False, 128))
                o = A(E, 0, 128) if k < 7 else A(E, 128, 256)
                it.append((o, A("DX", 128 * k, 128 * k + 128), A("G", j0 + k, j0 + 2048, 16), False, k in (6, 14), 128))
            mms(it, [sq("CA"), sq("CC"), sq("ONE"), ("DX", 0, 1920), ("G", j0, j0 + 2048)], [(E, 0, 256)])
            cur[0] = "t%d" % q
            th, zz = ("TH", z0, z0 + 256), ("Z", z0, z0 + 256)
            if q in THS:
                sa(th, (E, 0, 256), AF.Copy, bias=-7.5)
            else:
                ts(th, (E, 0, 256), -7.5, ALU.add)
            tt(zz, (E, 0, 256), th, ALU.subtract)
            sa(zz + (64, 128), zz + (64, 128), AF.Square)
            for b, ks in enumerate(SLOTS):
                D = BANKS[2 + b]
                za = z0 if b < 2 else z0 + 128
                it, rd = [], [("ZL", 128 * ks[0], 128 * ks[-1] + 128), ("Z", za, za + 128)]
                for x, k in enumerate(ks):
                    o = A(D, 128 * x, 128 * x + 128)
                    it.append((o, A("ZL", 128 * k, 128 * k + 128), A("Z", za, za + 128), True, k <= MINS, 128))
                    if k > MINS:
                        it.append((o, A("IDB", 0, 128), A("G", j0 + k, j0 + 2048, 16), False, True, 128))
                if ks[-1] > MINS:
                    rd += [sq("IDB"), ("G", j0, j0 + 2048)]
                n = 128 * len(ks)
                cur[0] = "d%d%d" % (q, b)
                mms(it, rd, [(D, 0, n)])
                rb = r0 + 128 * (ks[0] - 1)
                cur[0] = "r%d%d" % (q, b)
                if ks[-1] > MINS:
                    sa(("R", rb, rb + n), (D, 0, n), AF.Relu, bias=col(16) if b < 2 else col(8))
                else:
                    for x, k in enumerate(ks):
                        tt(("R", rb + 128 * x, rb + 128 * x + 128), (D, 128 * x, 128 * x + 128),
                           ("G", j0 + k, j0 + 2048), ALU.min, step1=16)
            for b, ks in enumerate(SLOTS):
                it, rd = [], [("S1", 0, 143), ("R", r0 + 128 * (ks[0] - 1), r0 + 128 * ks[-1])]
                if b == 0:
                    it.append((A(VB, 0, 128), A("RZ", 0, 128), A("G", j0, j0 + 2048, 16), True, False, 128))
                    it.append((A(VB, 0, 128), A("GC", 0, 128), A("Z", z0, z0 + 128), False, False, 128))
                    rd += [sq("RZ"), sq("GC"), ("G", j0, j0 + 2048), ("Z", z0, z0 + 128)]
                for k in ks:
                    rb = r0 + 128 * (k - 1)
                    it.append((A(VB, 0, 128), A("S1", 15 - k, 143 - k), A("R", rb, rb + 128), False, k == 15, 128))
                cur[0] = "s%d%d" % (q, b)
                mms(it, rd, [(VB, 0, 128)])
            cur[0] = "v%d" % q
            vq = (V, s0, s0 + 128)
            sa(vq, (VB, 0, 128), AF.Copy)
            mms([(A(VB, 128, 256), A("DF", 0, 128), A(*vq), True, True, 128)], [sq("DF"), vq], [(VB, 128, 256)])
            sa(("AB", s0, s0 + 128), (VB, 128, 256), AF.Abs)
            sa(("SG", s0, s0 + 128), ("AB", s0, s0 + 128), AF.Sign, bias=-64.5, acc=("ACC", q, q + 1))
            if q == 2:
                send(t, "vin", V, 128, "VIN%d" % t)
        cur[0] = "a"
        for qs in ((0, 1, 2), (3,)):
            mms([(A("e0", 0, 1), A("BO", 0, 128), A("ACC", q, q + 1), q == 0, q == 3, 256) for q in qs],
                [sq("BO"), ("ACC", qs[0], qs[-1] + 1)], [("e0", 0, 1)])
        for bank, mat, src in (("e1", "LW", V), ("d2", "S1", "SG")):
            mms([(A(bank, 0, 32), A(mat, 15 - r, 143 - r), A(src, r, 512, 16), r == 0, r == 15, 32) for r in range(16)],
                [(mat, 0, 143), (src, 0, 512)], [(bank, 0, 32)])
        Y = [("YW", 32 * i, 32 * i + 32) for i in range(10)]
        acol, hw, nw = ("e0", 0, 1), ("e1", 0, 32), ("d2", 0, 32)
        ts(Y[0], hw, acol, ALU.add, 512.0, ALU.mult)
        ts(Y[1], Y[0], 3584, ALU.bitwise_and)
        ts(Y[2], nw, -3.0, ALU.is_gt, 4096.0, ALU.mult)
        tt(Y[3], Y[2], ("II", 0, 32), ALU.add)
        tt(Y[4], Y[1], Y[3], ALU.add)
        cp((OF, 0, 32), Y[4])
        send(t, "oin", OF, 8, "OIN%d" % t)
        cur[0] = "n"
        ts(Y[5], hw, 37.0, ALU.mult, acol, ALU.add)
        ts(Y[6], Y[5], 4095, ALU.bitwise_and)
        ts(Y[7], nw, -3.0, ALU.is_lt, 8704.0, ALU.mult)
        tt(Y[8], Y[6], Y[7], ALU.add)
        tt(Y[9], Y[8], ("SI", 0, 32), ALU.max)
        ts((NX, 0, 32), Y[9], -8192.0, ALU.add)
        for c in range(0, 512, BCH):
            cur[0] = "b%d" % (c // 64)
            gather("V", ("GB", 16 * c, 16 * (c + BCH)), ("BT", 512, 4608), (C, c, c + BCH), bias=-2048.0)
        cur[0] = "m"
        ts(("CF", 0, 512), (C, 0, 512), -2048.0, ALU.add)
        for m in ORDER:
            a, b = 128 * m, 128 * m + 128
            it = [(A("d0", a, b), A("DB", 128 * k, 128 * k + 128), A("GB", 2048 * m + k, 2048 * m + 2048, 16), k == 0, False, 128)
                  for k in range(16)]
            it.append((A("d0", a, b), A("PP", 0, 128), A("SG", a, b), False, True, 128))
            mms(it, [("DB", 0, 2048), ("GB", 2048 * m, 2048 * m + 2048), sq("PP"), ("SG", a, b)], [("d0", a, b)])
        mms([(A("d1", 0, 512), A("I16", 0, 128), A("CF", 0, 512), True, False, 512),
             (A("d1", 0, 512), A("PN", 0, 128), A("SG", 0, 512), False, True, 512)],
            [sq("I16"), ("CF", 0, 512), sq("PN"), ("SG", 0, 512)], [("d1", 0, 512)])
        sa(("X2S", 0, 512), ("d1", 0, 512), AF.Copy)
        tt(("BT", 0, 512), ("d0", 0, 512), ("X2S", 0, 512), ALU.max)
        cur[0] = "o"
        scatter(("BT", 512, 8704), (OF, 0, 8), (C, 0, 128))
        scatter(("XT", 0, 8192), (OF, 0, 8), (V, 0, 128))
        cur[0] = "z"
        scatter(("BT", 512, 8704), ("OIN%d" % t, 0, 24), ("CIN%d" % t, 0, 384))
        scatter(("XT", 0, 8192), ("OIN%d" % t, 0, 24), ("VIN%d" % t, 0, 384))
        for m in ORDER:
            if t + 1 < NR:
                gather("V", ("C%d" % (t + 1), 128 * m, 128 * m + 128), ("BT", 0, 4608), (NX, 8 * m, 8 * m + 8))
            else:
                gather("V", ("YC", m, 512), ("BT", 0, 4608), (NX, 8 * m, 8 * m + 8), outstep=4)

    store("stx", T.yx[:], ("XT", 0, 4096), 7.0)
    store("stc", T.yc[:], ("YC", 0, 512), 3.0)
    if CAP is not None:
        CAP.append(ops)
        return
    run_queues(g, T, ops, sent)


def run_queues(g, T, ops, sent):
    n = len(ops)
    users = [[] for _ in range(n)]
    for i, o in enumerate(ops):
        for j in o["deps"]:
            users[j].append(i)
    wake = 0.12
    prio = [0.0] * n
    for i in range(n - 1, -1, -1):
        prio[i] = ops[i]["dur"] + ops[i]["lat"] + max([prio[u] + wake for u in users[i]] or [0.0])
    prio = [p + BON.get(o["tag"], 0.0) for p, o in zip(prio, ops)]
    left = [len(o["deps"]) for o in ops]
    ready = [0.0] * n
    free, cand = {}, {}
    for i, o in enumerate(ops):
        free[o["q"]] = 0.0
        cand.setdefault(o["q"], [])
        if left[i] == 0:
            cand[o["q"]].append(i)
    seq = []
    while len(seq) < n:
        best = None
        for q in sorted(cand):
            if cand[q]:
                s = min(max(ready[i], free[q]) for i in cand[q])
                if best is None or s < best[0]:
                    best = (s, q)
        s, q = best
        pick = max((i for i in cand[q] if max(ready[i], free[q]) <= s + LOOK), key=lambda i: (prio[i], -i))
        o = ops[pick]
        st = max(ready[pick], free[q])
        if q != "N":
            free[q] = st + o["dur"]
        end = st + o["dur"] + o["lat"]
        cand[q].remove(pick)
        seq.append(pick)
        for u in users[pick]:
            gap = wake
            if ops[u]["q"] == q:
                gap = 0.06 if ops[u]["deps"][pick] else 0.0
            ready[u] = max(ready[u], end + gap)
            left[u] -= 1
            if left[u] == 0:
                cand[ops[u]["q"]].append(u)

    eng = {"V": g.vector, "S": g.scalar, "P": g.tensor, "G": g, "Y": g.sync}
    cnt = {"V": 0, "S": 0, "P": 0, "G": 0}
    clock = {q: {} for q in free}
    know, done = {}, {}
    for i in seq:
        o = ops[i]
        q = o["q"]
        ck = clock[q]
        if q == "N":
            know[i] = {o["sem"]: o["val"]}
            done[i] = (o["sem"], o["val"])
            continue
        need = {}
        for j, hard in o["deps"].items():
            if hard:
                sem, val = done[j]
                if sem not in need or need[sem][0] < val:
                    need[sem] = (val, j)
        for sem, (val, j) in sorted(need.items(), key=lambda e: -e[1][1]):
            if ck.get(sem, 0) >= val:
                continue
            eng[q].wait_ge(T.sem[sem], val)
            for s2, v2 in know[j].items():
                ck[s2] = max(ck.get(s2, 0), v2)
        for th, inc in o["th"]:
            ins = th()
            if inc and o["sem"]:
                ins.then_inc(T.sem[o["sem"]], 16)
            elif inc:
                cnt[q] += 1
                ins.then_inc(T.sem["q" + q], 1)
        know[i] = dict(ck)
        done[i] = (o["sem"], o["val"]) if o["sem"] else ("q" + q, cnt.get(q, 0))
        know[i][done[i][0]] = done[i][1]
    for q in sorted(cnt):
        g.wait_ge(T.sem["q" + q], cnt[q])
    g.wait_ge(T.sem.loc, sent[0])
    for s in DMAS:
        g.wait_ge(T.sem[s], 16)
